import numpy as np, ml_dtypes
CORES = [24,40,56,80,88,96]
N = 6
import mx_ref
NC, G = 512, 4
C, C2 = np.float32(0.041), np.float32(0.037)
CNT = [[0,128,0,0,192,192],[96,0,0,128,96,192],[128,96,64,0,224,0],[0,64,96,224,0,128],[192,128,192,0,0,0],[96,96,160,160,0,0]]
OFF = [[sum(c[:e]) for e in range(N + 1)] for c in CNT]
BF = ml_dtypes.bfloat16
def cut(t, i, w=512):
    return t[:, w * i:w * i + w]
def tile(rs):
    return np.stack(rs, axis=2).reshape(128, -1).astype(BF)
def layer(w, X):
    out = []
    for i in range(G):
        for t in range(len(X)):
            p = mx_ref.matmul(mx_ref.quantize(cut(w, len(X) * i + t)), X[t])
            z = p if t == 0 else z + p
        out.append(z)
    return out
def act(Z):
    return [np.maximum(z, 0) * C for z in Z]
def setup_inputs(rng):
    def f(*shape):
        return mx_ref.flush((rng.standard_normal(shape, dtype=np.float32) * np.exp2(rng.integers(-2, 3, shape[:-1] + (1,)))).astype(BF))
    return {"x": f(N, 128, 4 * NC), "w1": f(N, 128, G * 512), "w2": f(N, 128, G * 512), "w3": f(N, 128, 512)}
def setup_inputs_blocks(rng):
    d = setup_inputs(rng)
    for k in ("x", "w3"): d[k] = mx_ref.spread(d[k], rng, 4)
    for k in ("w1", "w2"): d[k] = mx_ref.spread(d[k], rng, 2)
    return d
def setup_inputs_wide(rng):
    d = setup_inputs(rng)
    for k in ("x", "w1", "w2", "w3"): d[k] = mx_ref.flush((d[k].astype(np.float32) * np.exp2(rng.integers(-4, 5, (N, 1, 1))).astype(np.float32)).astype(BF))
    return d
def setup_inputs_zeros(rng):
    d = setup_inputs(rng); v = d["x"].reshape(N, 128, -1, 4).copy()
    v[np.broadcast_to((rng.random((N, 1, v.shape[2], 1)) < 0.33), v.shape)] = 0
    d["x"] = v.reshape(d["x"].shape)
    return d
def act2(Z):
    return [np.maximum(z, 0) * C2 for z in Z]
def reference(x, w1, w2, w3):
    h = [tile(act(layer(w1[j], [mx_ref.quantize(x[j])]))) for j in range(N)]
    g = []
    for e in range(N):
        t = np.concatenate([h[j][:, 4 * OFF[j][e]:4 * OFF[j][e + 1]] for j in range(N)], axis=1)
        g.append(tile(act2(layer(w2[e], [mx_ref.quantize(t)]))))
    y = np.zeros((N, 128, NC), np.float32)
    for j in range(N):
        back = []
        for e in range(N):
            a = sum(CNT[i][e] for i in range(j))
            back.append(g[e][:, 4 * a:4 * a + 4 * CNT[j][e]])
        y[j] = mx_ref.matmul(mx_ref.quantize(w3[j]), mx_ref.quantize(np.concatenate(back, axis=1)))
    return {"y": y}

@@ -1,0 +1,364 @@
+from concourse.bass import DstId, RemoteDMATransfer
+from concourse.mybir import dt, AluOpType, ActivationFunctionType
+
+NC = 512
+SIM_CORES = 112
+C1, C2 = 0.041, 0.037
+
+F8 = "float8_e4m3fn_x4"
+SCRATCH = {
+    "xt": ("sbuf", [128, 2048], "bfloat16"), "w1t": ("sbuf", [128, 2048], "bfloat16"),
+    "w2t": ("sbuf", [128, 2048], "bfloat16"), "w3t": ("sbuf", [128, 512], "bfloat16"),
+    "ht": ("sbuf", [128, 2048], "bfloat16"), "gt": ("sbuf", [128, 2048], "bfloat16"),
+    "yt": ("sbuf", [128, 512], "float32"),
+    "ps": ("psum", [128, 4096], "float32"),
+}
+for _n, _w in (("x", 512), ("w1", 512), ("w2", 512), ("w3", 128), ("h", 1024), ("g", 1024), ("ro", 512), ("rb", 512)):
+    SCRATCH["q" + _n] = ("sbuf", [128, _w], F8)
+    SCRATCH["s" + _n] = ("sbuf", [128, _w], "uint8")
+
+SEMAPHORES = (["lx0", "lx1", "lw10", "lw11", "lw2", "lw3", "qx0", "qx1", "qw10", "qw11", "qw2", "qw3",
+               "in0", "in1", "home0", "home1", "rin_o", "rin_b", "sent"]
+              + ["%s%d%d" % (p, c, i) for p in ("mh", "ah", "mg", "ag") for c in range(2) for i in range(4)]
+              + ["%s%d" % (p, c) for p in ("qh", "qg") for c in range(2)]
+              + ["%s%d%d" % (p, c, i) for p in ("my", "cy", "st") for c in range(2) for i in range(2)])
+
+
+def classes(dests, cnt):
+    out = {}
+    for d in dests:
+        out.setdefault(cnt[d], []).append(d)
+    return sorted(out.values(), key=lambda ds: -cnt[ds[0]] * len(ds))
+
+
+def halves(dests, cnt):
+    best = None
+    for m in range(1 << len(dests)):
+        s = [[d for k, d in enumerate(dests) if (m >> k & 1) == b] for b in (0, 1)]
+        cost = (max(len(classes(t, cnt)) for t in s), max(sum(cnt[d] for d in t) for t in s), s[0] == [])
+        if best is None or cost < best[0]:
+            best = (cost, s)
+    return [s for s in best[1] if s]
+
+
+def lay(pos, order, cnt, at):
+    for d in order:
+        pos[d] = at
+        at += cnt[d]
+    return at
+
+
+def windows(sets, cnt, a, b):
+    w = max(sum(cnt[d] for d in s) for s in sets)
+    return [(a, a + w), (b - w, b)][:len(sets)]
+
+
+def make_plan(T, topo):
+    CNT, cores = T.tables["CNT"], T.cores
+    n = len(cores)
+    far = [[i != j and not topo.may_write(cores[i], cores[j]) for j in range(n)] for i in range(n)]
+    P = []
+    for r in range(n):
+        p = {"far": far[r], "off": [sum(CNT[r][:e]) for e in range(n + 1)]}
+        oc = CNT[r]
+        fd = [e for e in range(n) if oc[e] and far[r][e]]
+        nd = [e for e in range(n) if oc[e] and not far[r][e] and e != r]
+        p["oc"], p["opos"] = oc, {}
+        own = p["own"] = oc[r]
+        p["osets"] = halves(fd, oc) if fd else []
+        if fd:
+            cut = lay(p["opos"], [d for s in p["osets"] for d in s], oc, 0)
+            p["onear"] = [[], classes(nd, oc)]
+        else:
+            cl = classes(nd, oc)
+            cut = sum(oc[d] for d in cl[0])
+            lay(p["opos"], cl[0], oc, 0)
+            p["onear"] = [cl[:1], cl[1:]]
+        lay(p["opos"], [d for c in p["onear"][0] + p["onear"][1] for d in c] if not fd else
+            [d for c in p["onear"][1] for d in c], oc, 0 if not fd else cut)
+        p["opos"][r] = NC - own
+        p["owin"] = windows(p["osets"], oc, 0, cut) if fd else []
+        p["hch"] = [(0, cut), (cut, NC)]
+        bc = p["bc"] = [CNT[i][r] for i in range(n)]
+        fs = [i for i in range(n) if bc[i] and far[r][i]]
+        ns = [i for i in range(n) if bc[i] and not far[r][i] and i != r]
+        if fs:
+            late = []
+            for i in sorted(ns, key=lambda i: bc[i]):
+                if sum(bc[k] for k in fs + late) < 128:
+                    late.append(i)
+        else:
+            late = [i for i in ns if any(far[i][e] and CNT[i][e] for e in range(n))]
+        early = [i for i in ns if i not in late]
+        p["bsets"] = halves(fs, bc) if fs else []
+        p["bnear"] = [classes(early, bc), classes(late, bc)]
+        p["bpos"] = {r: 0}
+        a = lay(p["bpos"], early, bc, own)
+        b = lay(p["bpos"], late, bc, a)
+        c = lay(p["bpos"], [d for s in p["bsets"] for d in s], bc, b)
+        p["bwin"] = windows(p["bsets"], bc, b, c) if fs else []
+        p["gch"] = [(0, a), (a, NC)]
+        p["inch"] = [0 if i in early else 1 for i in range(n)]
+        p["apos"] = {}
+        a = lay(p["apos"], fd, oc, 0)
+        lay(p["apos"], nd, oc, a)
+        p["apos"][r] = NC - own
+        p["ych"] = [(a, NC), (0, a)] if fd else [(0, NC)]
+        if fd or fs:
+            probe = (fd + fs)[0]
+            p["relays"] = sorted([c for c in range(SIM_CORES) if topo.chip(c) == topo.chip(cores[r])
+                                  and c != cores[r] and topo.may_write(c, cores[probe])],
+                                 key=lambda c: (topo.die(c) != topo.die(cores[r]), c))
+        else:
+            p["relays"] = []
+        P.append(p)
+    return P
+
+
+def runs(pos, p, a, b):
+    out = []
+    for at, d in sorted((at, d) for d, at in pos.items() if p["oc"][d]):
+        lo, hi = max(a, at), min(b, at + p["oc"][d])
+        if lo >= hi:
+            continue
+        o = p["off"][d] + lo - at
+        if out and out[-1][0] + out[-1][2] == lo and out[-1][1] + out[-1][2] == o:
+            out[-1][2] += hi - lo
+        else:
+            out.append([lo, o, hi - lo])
+    return out
+
+
+def ones(m):
+    return bin(m).count("1")
+
+
+def deal(mask, k):
+    bits = [b for b in range(mask.bit_length()) if mask >> b & 1]
+    return [sum(1 << b for b in bits[i::k]) for i in range(k)]
+
+
+def view(T, kind, name, a, b):
+    if kind == 0:
+        return T["q" + name][:, a:b].bitcast(dt.uint8)
+    return T["s" + name][:, a:b]
+
+
+def send(g, T, topo, core, kind, items, sent):
+    k = len(items)
+    ms = [deal(topo.mask(core, it[0]), k)[i] for i, it in enumerate(items)]
+    sent[0] += sum(ones(m) for m in ms)
+    if k == 1:
+        dst, sem, (sb, sa), (tb, ta), w = items[0]
+        rid, pid, _ = topo.addr(dst)
+        g.remote_dma(view(T, kind, tb, ta, ta + w), view(T, kind, sb, sa, sa + w), T.sem[sem], T.sem.sent, pid, rid, ms[0])
+        return
+    tr = []
+    for m, (dst, sem, (sb, sa), (tb, ta), w) in zip(ms, items):
+        rid, pid, _ = topo.addr(dst)
+        tr.append(RemoteDMATransfer(dst_ids=[DstId(rid=rid, pnc=pid)], dma_engine_mask=m, remote_sem=T.sem[sem],
+                                    src=view(T, kind, sb, sa, sa + w), dst=view(T, kind, tb, ta, ta + w)))
+    g.remote_dma_fused(tr, local_sem=T.sem.sent)
+
+
+def target(P, phase, r, d):
+    q = P[d]
+    if phase == "o":
+        return "in%d" % q["inch"][r], "h", NC - q["own"] + q["bpos"][r]
+    return "home%d" % (1 if q["far"][r] else 0), "g", q["own"] + q["apos"][r]
+
+
+def source(P, phase, r):
+    p = P[r]
+    return (p["opos"], p["oc"], 0, "h") if phase == "o" else (p["bpos"], p["bc"], NC, "g")
+
+
+def near_calls(P, phase, r, chunk):
+    pos, cnt, base, buf = source(P, phase, r)
+    out = []
+    for cl in P[r]["onear" if phase == "o" else "bnear"][chunk]:
+        out.append([(d,) + (target(P, phase, r, d),) + ((buf, base + pos[d]), cnt[d]) for d in cl])
+    return out
+
+
+def arrivals(P, topo, cores, phase, d, sem):
+    tot = 0
+    for r in range(len(P)):
+        if r == d or not source(P, phase, r)[1][d] or target(P, phase, r, d)[0] != sem:
+            continue
+        p, cnt = P[r], source(P, phase, r)[1]
+        if p["far"][d]:
+            for s, st in enumerate(p["osets" if phase == "o" else "bsets"]):
+                if d in st:
+                    cl = [c for c in classes(st, cnt) if d in c][0]
+                    for kind in (0, 1):
+                        tot += ones(topo.mask(p["relays"][2 * s + kind], cores[d])) // len(cl)
+        else:
+            cl = [c for ch in p["onear" if phase == "o" else "bnear"] for c in ch if d in c][0]
+            tot += 2 * (ones(topo.mask(cores[r], cores[d])) // len(cl))
+    return tot
+
+
+def relay_core(g, core, T, topo, P, r):
+    p, cores, sent = P[r], T.cores, [0]
+    k = p["relays"].index(core)
+    pair, kind = k // 2, k % 2
+    for phase in ("o", "b"):
+        sets = p["osets" if phase == "o" else "bsets"]
+        if pair >= len(sets):
+            continue
+        pos, cnt, base, buf = source(P, phase, r)
+        win = p["owin" if phase == "o" else "bwin"][pair]
+        g.wait_ge(T.sem["rin_" + phase], ones(deal(topo.mask(cores[r], core), len(sets))[pair]))
+        for cl in classes(sets[pair], cnt):
+            items = []
+            for d in cl:
+                sem, tb, ta = target(P, phase, r, d)
+                items.append((cores[d], sem, ("r" + phase, pos[d] - win[0]), (tb, ta), cnt[d]))
+            send(g, T, topo, core, kind, items, sent)
+    if sent[0]:
+        g.wait_ge(T.sem.sent, sent[0])
+
+
+def rank_core(g, core, T, topo, P, r):
+    p, cores, sent, S = P[r], T.cores, [0], T.sem
+    hch, gch, own = p["hch"], p["gch"], p["own"]
+    relu = ActivationFunctionType.Relu
+
+    nx = []
+    for c in range(2):
+        rs = runs(p["opos"], p, *hch[c])
+        nx.append(16 * len(rs))
+        for at, o, w in rs:
+            g.sync.dma_start(T.xt[:, 4 * at:4 * (at + w)], T.x[:, 4 * o:4 * (o + w)]).then_inc(S["lx%d" % c], 16)
+        g.scalar.dma_start(T.w1t[:, 1024 * c:1024 * (c + 1)], T.w1[:, 1024 * c:1024 * (c + 1)]).then_inc(S["lw1%d" % c], 16)
+    g.sync.dma_start(T.w2t[:], T.w2[:]).then_inc(S.lw2, 16)
+    g.sync.dma_start(T.w3t[:], T.w3[:]).then_inc(S.lw3, 16)
+
+    def quant(name, tile, a, b, sem, at=None):
+        at = a if at is None else at
+        g.vector.quantize_mx(T["q" + name][:, at:at + b - a], T["s" + name][:, at:at + b - a],
+                             T[tile][:, 4 * a:4 * b]).then_inc(S[sem], 1)
+
+    def products(w, buf, at, n, c, sem, gate=None):
+        for i in range(4):
+            if gate and i in gate:
+                g.tensor.wait_ge(S[gate[i]], 1)
+            bank = 512 * (4 * c + i)
+            g.tensor.matmul_mx(T.ps[:, bank:bank + n], T["q" + w][:, 128 * i:128 * i + 128], T["s" + w][:, 128 * i:128 * i + 128],
+                               T["q" + buf][:, at:at + n], T["s" + buf][:, at:at + n], True, True).then_inc(S["%s%d%d" % (sem, c, i)], 1)
+
+    def drain(tile, a, b, c, const, m, s):
+        for i in range(4):
+            bank = 512 * (4 * c + i)
+            out, src = T[tile][:, 4 * a + i:4 * b:4], T.ps[:, bank:bank + b - a]
+            q = g.vector if i % 2 else g.scalar
+            q.wait_ge(S["%s%d%d" % (m, c, i)], 1)
+            if i % 2:
+                g.vector.tensor_scalar(out, src, 0.0, const, AluOpType.max, AluOpType.mult).then_inc(S["%s%d%d" % (s, c, i)], 1)
+            else:
+                g.scalar.activation(out, src, relu, scale=const).then_inc(S["%s%d%d" % (s, c, i)], 1)
+        for i in range(4):
+            g.vector.wait_ge(S["%s%d%d" % (s, c, i)], 1)
+
+    g.vector.wait_ge(S.lx0, nx[0])
+    quant("x", "xt", hch[0][0], hch[0][1], "qx0")
+    for c in range(2):
+        g.vector.wait_ge(S["lw1%d" % c], 16)
+        quant("w1", "w1t", 256 * c, 256 * c + 256, "qw1%d" % c)
+    g.tensor.wait_ge(S.qx0, 1)
+    products("w1", "x", hch[0][0], hch[0][1] - hch[0][0], 0, "mh", {0: "qw10", 2: "qw11"})
+    drain("ht", hch[0][0], hch[0][1], 0, C1, "mh", "ah")
+    quant("h", "ht", hch[0][0], hch[0][1], "qh0")
+    g.vector.wait_ge(S.lx1, nx[1])
+    quant("x", "xt", hch[1][0], hch[1][1], "qx1")
+    g.tensor.wait_ge(S.qx1, 1)
+    products("w1", "x", hch[1][0], hch[1][1] - hch[1][0], 1, "mh")
+    drain("ht", hch[1][0], hch[1][1], 1, C1, "mh", "ah")
+    quant("h", "ht", hch[1][0], hch[1][1], "qh1")
+    g.vector.wait_ge(S.lw2, 16)
+    quant("w2", "w2t", 0, 512, "qw2")
+    g.vector.wait_ge(S.lw3, 16)
+    quant("w3", "w3t", 0, 128, "qw3")
+
+    def far_send(phase):
+        sets = p["osets" if phase == "o" else "bsets"]
+        pos, cnt, base, buf = source(P, phase, r)
+        for kind in (0, 1):
+            items = []
+            for s, (a, b) in enumerate(p["owin" if phase == "o" else "bwin"]):
+                items.append((p["relays"][2 * s + kind], "rin_" + phase, (buf, base + a), ("r" + phase, 0), b - a))
+            if items:
+                send(g, T, topo, core, kind, items, sent)
+
+    def near_send(phase, chunk):
+        for call in near_calls(P, phase, r, chunk):
+            for kind in (0, 1):
+                send(g, T, topo, core, kind, [(cores[d], sem, src, (tb, ta), w) for d, (sem, tb, ta), src, w in call], sent)
+
+    g.wait_ge(S.qh0, 1)
+    far_send("o")
+    near_send("o", 0)
+    g.wait_ge(S.qh1, 1)
+    near_send("o", 1)
+
+    g.tensor.wait_ge(S.qw2, 1)
+    for c in range(2):
+        a, b = gch[c]
+        g.tensor.wait_ge(S["qh%d" % c], 1)
+        if c == 0:
+            g.tensor.wait_ge(S.qh1, 1)
+        g.tensor.wait_ge(S["in%d" % c], arrivals(P, topo, cores, "o", r, "in%d" % c))
+        products("w2", "h", NC - own + a, b - a, c, "mg")
+        drain("gt", a, b, c, C2, "mg", "ag")
+        quant("g", "gt", a, b, "qg%d" % c, NC + a)
+    if p["bsets"]:
+        g.wait_ge(S.qg1, 1)
+        far_send("b")
+        g.wait_ge(S.qg0, 1)
+        near_send("b", 0)
+        near_send("b", 1)
+    else:
+        for c in range(2):
+            g.wait_ge(S["qg%d" % c], 1)
+            near_send("b", c)
+
+    g.tensor.wait_ge(S.qw3, 1)
+    for c, (a, b) in enumerate(p["ych"]):
+        g.tensor.wait_ge(S["qg%d" % c], 1)
+        if c == 0 and len(p["ych"]) == 1:
+            g.tensor.wait_ge(S.qg1, 1)
+        g.tensor.wait_ge(S["home%d" % c], arrivals(P, topo, cores, "b", r, "home%d" % c))
+        parts = [(a, b)]
+        if b - a >= 256:
+            edges = [at for at in p["apos"].values() if a + 128 <= at <= b - 128] or [(a + b) // 2]
+            mid = min(edges, key=lambda at: abs(2 * at - a - b))
+            parts = [(a, mid), (mid, b)]
+        for i, (lo, hi) in enumerate(parts):
+            bank = 512 * (4 * c + i)
+            k = "%d%d" % (c, i)
+            g.tensor.matmul_mx(T.ps[:, bank:bank + hi - lo], T.qw3[:], T.sw3[:], T.qg[:, own + lo:own + hi],
+                               T.sg[:, own + lo:own + hi], True, True).then_inc(S["my" + k], 1)
+            cp, st = (g.vector, g.sync) if i else (g.scalar, g.scalar)
+            cp.wait_ge(S["my" + k], 1)
+            if i:
+                g.vector.tensor_copy(T.yt[:, lo:hi], T.ps[:, bank:bank + hi - lo]).then_inc(S["cy" + k], 1)
+            else:
+                g.scalar.activation(T.yt[:, lo:hi], T.ps[:, bank:bank + hi - lo], ActivationFunctionType.Copy).then_inc(S["cy" + k], 1)
+            st.wait_ge(S["cy" + k], 1)
+            rs = runs(p["apos"], p, lo, hi)
+            for at, o, w in rs:
+                st.dma_start(T.y[:, o:o + w], T.yt[:, at:at + w]).then_inc(S["st" + k], 16)
+            g.wait_ge(S["st" + k], 16 * len(rs))
+    g.wait_ge(S.sent, sent[0])
+
+
+def rank_program(g, core, T, topo):
+    P = make_plan(T, topo)
+    r = T.rank_of(core)
+    if r is not None:
+        rank_core(g, core, T, topo, P, r)
+        return
+    for j in range(len(P)):
+        if core in P[j]["relays"][:4]:
+            relay_core(g, core, T, topo, P, j)

@@ -5,6 +5,37 @@ NC = 512
 SIM_CORES = 112
 C1, C2 = 0.041, 0.037
 
+OUT = [
+    [[[[5]]], [[[4]]], [[[1]]]],
+    [[[[5]]], [[[3]]], [[[0]], [[4]]]],
+    [[[[0]]], [[[4]]], [[[1]]]],
+    [[[[2]], [[1]]], [[[5]]]],
+    [[[[1]]], [[[2]]], [[[0]]]],
+    [[[[2]]], [[[0, 1]]], [[[3]]]],
+]
+BACK = [
+    [[[[4]]], [[[2]]], [[[1]], [[5]]]],
+    [[[[4]]], [[[0]], [[2]]], [[[5], [3]]]],
+    [[[[4]]], [[[5]], [[3]]]],
+    [[], [[[5]]], [[[1]]]],
+    [[[[2]]], [[[1]], [[0]]]],
+    [[[[3]]], [[[1]]], [[[0]]]],
+]
+SENDS = [
+    [(0, 0), (2, 0), (2, 1), (1, 0)],
+    [(0, 0), (2, 0), (1, 1), (1, 0)],
+    [(0, 0), (1, 0), (1, 1)],
+    [(2, 0), (1, 0)],
+    [(0, 0), (1, 1), (1, 0)],
+    [(1, 0), (2, 0), (0, 0)],
+]
+VIA_O = [[], [], [0], [], [], []]
+VIA_B = [[4], [], [], [], [], []]
+FIRST_O = [0, 1, 0, 0, 1, 1]
+FIRST_B = [1, 1, 0, 0, 1, 1]
+VEC_H0, VEC_H, VEC_G = (1,), (1, 3), (2,)
+MAXCH = 3
+
 F8 = "float8_e4m3fn_x4"
 SCRATCH = {
     "xt": ("sbuf", [128, 2048], "bfloat16"), "w1t": ("sbuf", [128, 2048], "bfloat16"),
@@ -17,10 +48,9 @@ for _n, _w in (("x", 512), ("w1", 512), ("w2", 512), ("w3", 128), ("h", 1024), (
     SCRATCH["q" + _n] = ("sbuf", [128, _w], F8)
     SCRATCH["s" + _n] = ("sbuf", [128, _w], "uint8")
 
-SEMAPHORES = (["lx0", "lx1", "lw10", "lw11", "lw2", "lw3", "qx0", "qx1", "qw10", "qw11", "qw2", "qw3",
-               "in0", "in1", "home0", "home1", "rin_o", "rin_b", "sent"]
-              + ["%s%d%d" % (p, c, i) for p in ("mh", "ah", "mg", "ag") for c in range(2) for i in range(4)]
-              + ["%s%d" % (p, c) for p in ("qh", "qg") for c in range(2)]
+SEMAPHORES = (["lw10", "lw11", "lw2", "lw3", "qw10", "qw11", "qw2", "qw3", "home0", "home1", "rin_o", "rin_b", "sent"]
+              + ["%s%d" % (p, c) for p in ("lx", "qx", "qh", "qg", "in") for c in range(MAXCH)]
+              + ["%s%d%d" % (p, c, i) for p in ("mh", "ah", "mg", "ag") for c in range(MAXCH) for i in range(4)]
               + ["%s%d%d" % (p, c, i) for p in ("my", "cy", "st") for c in range(2) for i in range(2)])
 
 
@@ -31,94 +61,72 @@ def classes(dests, cnt):
     return sorted(out.values(), key=lambda ds: -cnt[ds[0]] * len(ds))
 
 
-def halves(dests, cnt):
-    best = None
-    for m in range(1 << len(dests)):
-        s = [[d for k, d in enumerate(dests) if (m >> k & 1) == b] for b in (0, 1)]
-        cost = (max(len(classes(t, cnt)) for t in s), max(sum(cnt[d] for d in t) for t in s), s[0] == [])
-        if best is None or cost < best[0]:
-            best = (cost, s)
-    return [s for s in best[1] if s]
-
-
-def lay(pos, order, cnt, at):
-    for d in order:
-        pos[d] = at
-        at += cnt[d]
-    return at
-
-
-def windows(sets, cnt, a, b):
-    w = max(sum(cnt[d] for d in s) for s in sets)
-    return [(a, a + w), (b - w, b)][:len(sets)]
+def lay_out(chunks, cnt, relayed, at, first, last):
+    pos, bounds, calls, pair = {}, [], [], 0
+    start = at
+    at += first
+    for c, chunk in enumerate(chunks):
+        calls.append([])
+        for call in chunk:
+            for tr in call:
+                for d in tr:
+                    pos[d] = at
+                    at += cnt[d]
+            if relayed[call[0][0]]:
+                w = max(sum(cnt[d] for d in tr) for tr in call)
+                items = []
+                for tr in call:
+                    items.append((pair, min(pos[tr[0]], at - w), w, tr))
+                    pair += 1
+                calls[-1].append((True, items))
+            else:
+                calls[-1].append((False, [tr[0] for tr in call]))
+        if c == len(chunks) - 1:
+            at += last
+        bounds.append((start, at))
+        start = at
+    return pos, bounds, calls
 
 
 def make_plan(T, topo):
     CNT, cores = T.tables["CNT"], T.cores
     n = len(cores)
-    far = [[i != j and not topo.may_write(cores[i], cores[j]) for j in range(n)] for i in range(n)]
     P = []
     for r in range(n):
-        p = {"far": far[r], "off": [sum(CNT[r][:e]) for e in range(n + 1)]}
-        oc = CNT[r]
-        fd = [e for e in range(n) if oc[e] and far[r][e]]
-        nd = [e for e in range(n) if oc[e] and not far[r][e] and e != r]
-        p["oc"], p["opos"] = oc, {}
-        own = p["own"] = oc[r]
-        p["osets"] = halves(fd, oc) if fd else []
-        if fd:
-            cut = lay(p["opos"], [d for s in p["osets"] for d in s], oc, 0)
-            p["onear"] = [[], classes(nd, oc)]
-        else:
-            cl = classes(nd, oc)
-            cut = sum(oc[d] for d in cl[0])
-            lay(p["opos"], cl[0], oc, 0)
-            p["onear"] = [cl[:1], cl[1:]]
-        lay(p["opos"], [d for c in p["onear"][0] + p["onear"][1] for d in c] if not fd else
-            [d for c in p["onear"][1] for d in c], oc, 0 if not fd else cut)
-        p["opos"][r] = NC - own
-        p["owin"] = windows(p["osets"], oc, 0, cut) if fd else []
-        p["hch"] = [(0, cut), (cut, NC)]
-        bc = p["bc"] = [CNT[i][r] for i in range(n)]
-        fs = [i for i in range(n) if bc[i] and far[r][i]]
-        ns = [i for i in range(n) if bc[i] and not far[r][i] and i != r]
-        if fs:
-            late = []
-            for i in sorted(ns, key=lambda i: bc[i]):
-                if sum(bc[k] for k in fs + late) < 128:
-                    late.append(i)
-        else:
-            late = [i for i in ns if any(far[i][e] and CNT[i][e] for e in range(n))]
-        early = [i for i in ns if i not in late]
-        p["bsets"] = halves(fs, bc) if fs else []
-        p["bnear"] = [classes(early, bc), classes(late, bc)]
-        p["bpos"] = {r: 0}
-        a = lay(p["bpos"], early, bc, own)
-        b = lay(p["bpos"], late, bc, a)
-        c = lay(p["bpos"], [d for s in p["bsets"] for d in s], bc, b)
-        p["bwin"] = windows(p["bsets"], bc, b, c) if fs else []
-        p["gch"] = [(0, a), (a, NC)]
-        p["inch"] = [0 if i in early else 1 for i in range(n)]
-        p["apos"] = {}
-        a = lay(p["apos"], fd, oc, 0)
-        lay(p["apos"], nd, oc, a)
-        p["apos"][r] = NC - own
-        p["ych"] = [(a, NC), (0, a)] if fd else [(0, NC)]
-        if fd or fs:
-            probe = (fd + fs)[0]
-            p["relays"] = sorted([c for c in range(SIM_CORES) if topo.chip(c) == topo.chip(cores[r])
-                                  and c != cores[r] and topo.may_write(c, cores[probe])],
-                                 key=lambda c: (topo.die(c) != topo.die(cores[r]), c))
-        else:
-            p["relays"] = []
+        far = [i != r and not topo.may_write(cores[r], cores[i]) for i in range(n)]
+        oc, bc, own = CNT[r], [CNT[i][r] for i in range(n)], CNT[r][r]
+        p = {"far": far, "own": own, "off": [sum(oc[:e]) for e in range(n + 1)], "o": {}, "b": {}}
+        o, b = p["o"], p["b"]
+        o["cnt"], o["base"], o["buf"] = oc, 0, "h"
+        o["pos"], o["ch"], o["calls"] = lay_out(OUT[r], oc, [far[i] or i in VIA_O[r] for i in range(n)], 0, 0, own)
+        o["pos"][r] = NC - own
+        b["cnt"], b["base"], b["buf"] = bc, NC, "g"
+        b["pos"], b["ch"], b["calls"] = lay_out(BACK[r], bc, [far[i] or i in VIA_B[r] for i in range(n)], 0, own, 0)
+        b["pos"][r] = 0
+        b["of"] = {d: c for c, chunk in enumerate(BACK[r]) for call in chunk for tr in call for d in tr}
+        p["apos"], at, cut = {}, 0, 0
+        for f in (True, False):
+            for d in range(n):
+                if oc[d] and d != r and far[d] == f:
+                    p["apos"][d] = at
+                    at += oc[d]
+            cut = at if f else cut
+        p["apos"][r] = at
+        p["ych"] = [(cut, NC), (0, cut)] if cut else [(0, NC)]
+        probe = [i for i in range(n) if far[i]][0]
+        rel = sorted([c for c in range(SIM_CORES) if topo.chip(c) == topo.chip(cores[r])
+                      and c != cores[r] and topo.may_write(c, cores[probe])],
+                     key=lambda c: (topo.die(c) == topo.die(cores[r]), c))
+        o["relays"] = rel[2 * FIRST_O[r]:] + rel[:2 * FIRST_O[r]]
+        b["relays"] = rel[2 * FIRST_B[r]:] + rel[:2 * FIRST_B[r]]
         P.append(p)
     return P
 
 
 def runs(pos, p, a, b):
     out = []
-    for at, d in sorted((at, d) for d, at in pos.items() if p["oc"][d]):
-        lo, hi = max(a, at), min(b, at + p["oc"][d])
+    for at, d in sorted((at, d) for d, at in pos.items() if p["o"]["cnt"][d]):
+        lo, hi = max(a, at), min(b, at + p["o"]["cnt"][d])
         if lo >= hi:
             continue
         o = p["off"][d] + lo - at
@@ -164,75 +172,62 @@ def send(g, T, topo, core, kind, items, sent):
 def target(P, phase, r, d):
     q = P[d]
     if phase == "o":
-        return "in%d" % q["inch"][r], "h", NC - q["own"] + q["bpos"][r]
+        return "in%d" % q["b"]["of"][r], "h", NC - q["own"] + q["b"]["pos"][r]
     return "home%d" % (1 if q["far"][r] else 0), "g", q["own"] + q["apos"][r]
-
-
-def source(P, phase, r):
-    p = P[r]
-    return (p["opos"], p["oc"], 0, "h") if phase == "o" else (p["bpos"], p["bc"], NC, "g")
-
-
-def near_calls(P, phase, r, chunk):
-    pos, cnt, base, buf = source(P, phase, r)
-    out = []
-    for cl in P[r]["onear" if phase == "o" else "bnear"][chunk]:
-        out.append([(d,) + (target(P, phase, r, d),) + ((buf, base + pos[d]), cnt[d]) for d in cl])
-    return out
 
 
 def arrivals(P, topo, cores, phase, d, sem):
     tot = 0
     for r in range(len(P)):
-        if r == d or not source(P, phase, r)[1][d] or target(P, phase, r, d)[0] != sem:
+        if r == d or not P[r][phase]["cnt"][d] or target(P, phase, r, d)[0] != sem:
             continue
-        p, cnt = P[r], source(P, phase, r)[1]
-        if p["far"][d]:
-            for s, st in enumerate(p["osets" if phase == "o" else "bsets"]):
-                if d in st:
-                    cl = [c for c in classes(st, cnt) if d in c][0]
-                    for kind in (0, 1):
-                        tot += ones(topo.mask(p["relays"][2 * s + kind], cores[d])) // len(cl)
-        else:
-            cl = [c for ch in p["onear" if phase == "o" else "bnear"] for c in ch if d in c][0]
-            tot += 2 * (ones(topo.mask(cores[r], cores[d])) // len(cl))
+        for calls in P[r][phase]["calls"]:
+            for relayed, items in calls:
+                if not relayed and d in items:
+                    tot += 2 * (ones(topo.mask(cores[r], cores[d])) // len(items))
+                for pair, lo, w, tr in items if relayed else []:
+                    if d in tr:
+                        cl = [c for c in classes(tr, P[r][phase]["cnt"]) if d in c][0]
+                        for kind in (0, 1):
+                            tot += ones(topo.mask(P[r][phase]["relays"][2 * pair + kind], cores[d])) // len(cl)
     return tot
 
 
 def relay_core(g, core, T, topo, P, r):
     p, cores, sent = P[r], T.cores, [0]
-    k = p["relays"].index(core)
-    pair, kind = k // 2, k % 2
     for phase in ("o", "b"):
-        sets = p["osets" if phase == "o" else "bsets"]
-        if pair >= len(sets):
-            continue
-        pos, cnt, base, buf = source(P, phase, r)
-        win = p["owin" if phase == "o" else "bwin"][pair]
-        g.wait_ge(T.sem["rin_" + phase], ones(deal(topo.mask(cores[r], core), len(sets))[pair]))
-        for cl in classes(sets[pair], cnt):
-            items = []
-            for d in cl:
-                sem, tb, ta = target(P, phase, r, d)
-                items.append((cores[d], sem, ("r" + phase, pos[d] - win[0]), (tb, ta), cnt[d]))
-            send(g, T, topo, core, kind, items, sent)
+        ph = p[phase]
+        k = ph["relays"].index(core)
+        for relayed, items in [c for cs in ph["calls"] for c in cs]:
+            for i, (pair, lo, w, tr) in enumerate(items if relayed else []):
+                if pair != k // 2:
+                    continue
+                g.wait_ge(T.sem["rin_" + phase], ones(deal(topo.mask(cores[r], core), len(items))[i]))
+                for cl in classes(tr, ph["cnt"]):
+                    out = []
+                    for d in cl:
+                        sem, tb, ta = target(P, phase, r, d)
+                        out.append((cores[d], sem, ("r" + phase, ph["pos"][d] - lo), (tb, ta), ph["cnt"][d]))
+                    send(g, T, topo, core, k % 2, out, sent)
     if sent[0]:
         g.wait_ge(T.sem.sent, sent[0])
 
 
 def rank_core(g, core, T, topo, P, r):
     p, cores, sent, S = P[r], T.cores, [0], T.sem
-    hch, gch, own = p["hch"], p["gch"], p["own"]
+    hch, gch, own = p["o"]["ch"], p["b"]["ch"], p["own"]
     relu = ActivationFunctionType.Relu
 
     nx = []
-    for c in range(2):
-        rs = runs(p["opos"], p, *hch[c])
+    for c in range(len(hch)):
+        rs = runs(p["o"]["pos"], p, *hch[c])
         nx.append(16 * len(rs))
         for at, o, w in rs:
             g.sync.dma_start(T.xt[:, 4 * at:4 * (at + w)], T.x[:, 4 * o:4 * (o + w)]).then_inc(S["lx%d" % c], 16)
+    for c in range(2):
         g.scalar.dma_start(T.w1t[:, 1024 * c:1024 * (c + 1)], T.w1[:, 1024 * c:1024 * (c + 1)]).then_inc(S["lw1%d" % c], 16)
     g.sync.dma_start(T.w2t[:], T.w2[:]).then_inc(S.lw2, 16)
+    g.sync.wait_ge(S.qg0, 1)
     g.sync.dma_start(T.w3t[:], T.w3[:]).then_inc(S.lw3, 16)
 
     def quant(name, tile, a, b, sem, at=None):
@@ -240,94 +235,92 @@ def rank_core(g, core, T, topo, P, r):
         g.vector.quantize_mx(T["q" + name][:, at:at + b - a], T["s" + name][:, at:at + b - a],
                              T[tile][:, 4 * a:4 * b]).then_inc(S[sem], 1)
 
-    def products(w, buf, at, n, c, sem, gate=None):
+    freed = []
+
+    def bank(i):
+        return 512 * (4 * (len(freed) % 2) + i)
+
+    def take():
+        if len(freed) >= 2:
+            g.tensor.wait_ge(S[freed[-2]], 1)
+
+    def layer(w, buf, at, tile, a, b, const, m, s, q, vec, gate=None, ahead=None):
+        n = b - a
+        take()
         for i in range(4):
             if gate and i in gate:
                 g.tensor.wait_ge(S[gate[i]], 1)
-            bank = 512 * (4 * c + i)
-            g.tensor.matmul_mx(T.ps[:, bank:bank + n], T["q" + w][:, 128 * i:128 * i + 128], T["s" + w][:, 128 * i:128 * i + 128],
-                               T["q" + buf][:, at:at + n], T["s" + buf][:, at:at + n], True, True).then_inc(S["%s%d%d" % (sem, c, i)], 1)
-
-    def drain(tile, a, b, c, const, m, s):
+            g.tensor.matmul_mx(T.ps[:, bank(i):bank(i) + n], T["q" + w][:, 128 * i:128 * i + 128], T["s" + w][:, 128 * i:128 * i + 128],
+                               T["q" + buf][:, at:at + n], T["s" + buf][:, at:at + n], True, True).then_inc(S["%s%d" % (m, i)], 1)
+        if ahead:
+            ahead()
         for i in range(4):
-            bank = 512 * (4 * c + i)
-            out, src = T[tile][:, 4 * a + i:4 * b:4], T.ps[:, bank:bank + b - a]
-            q = g.vector if i % 2 else g.scalar
-            q.wait_ge(S["%s%d%d" % (m, c, i)], 1)
-            if i % 2:
-                g.vector.tensor_scalar(out, src, 0.0, const, AluOpType.max, AluOpType.mult).then_inc(S["%s%d%d" % (s, c, i)], 1)
+            out, src = T[tile][:, 4 * a + i:4 * b:4], T.ps[:, bank(i):bank(i) + n]
+            e = g.vector if i in vec else g.scalar
+            e.wait_ge(S["%s%d" % (m, i)], 1)
+            if i in vec:
+                g.vector.tensor_scalar(out, src, 0.0, const, AluOpType.max, AluOpType.mult).then_inc(S["%s%d" % (s, i)], 1)
             else:
-                g.scalar.activation(out, src, relu, scale=const).then_inc(S["%s%d%d" % (s, c, i)], 1)
+                g.scalar.activation(out, src, relu, scale=const).then_inc(S["%s%d" % (s, i)], 1)
         for i in range(4):
-            g.vector.wait_ge(S["%s%d%d" % (s, c, i)], 1)
+            g.vector.wait_ge(S["%s%d" % (s, i)], 1)
+        freed.append(q)
 
-    g.vector.wait_ge(S.lx0, nx[0])
-    quant("x", "xt", hch[0][0], hch[0][1], "qx0")
+    def quant_x(c):
+        if c < len(hch):
+            g.vector.wait_ge(S["lx%d" % c], nx[c])
+            quant("x", "xt", hch[c][0], hch[c][1], "qx%d" % c)
+
+    quant_x(0)
     for c in range(2):
         g.vector.wait_ge(S["lw1%d" % c], 16)
         quant("w1", "w1t", 256 * c, 256 * c + 256, "qw1%d" % c)
-    g.tensor.wait_ge(S.qx0, 1)
-    products("w1", "x", hch[0][0], hch[0][1] - hch[0][0], 0, "mh", {0: "qw10", 2: "qw11"})
-    drain("ht", hch[0][0], hch[0][1], 0, C1, "mh", "ah")
-    quant("h", "ht", hch[0][0], hch[0][1], "qh0")
-    g.vector.wait_ge(S.lx1, nx[1])
-    quant("x", "xt", hch[1][0], hch[1][1], "qx1")
-    g.tensor.wait_ge(S.qx1, 1)
-    products("w1", "x", hch[1][0], hch[1][1] - hch[1][0], 1, "mh")
-    drain("ht", hch[1][0], hch[1][1], 1, C1, "mh", "ah")
-    quant("h", "ht", hch[1][0], hch[1][1], "qh1")
+    for c, (a, b) in enumerate(hch):
+        g.tensor.wait_ge(S["qx%d" % c], 1)
+        layer("w1", "x", a, "ht", a, b, C1, "mh%d" % c, "ah%d" % c, "qh%d" % c, VEC_H if c else VEC_H0,
+              gate={} if c else {0: "qw10", 2: "qw11"}, ahead=lambda: quant_x(c + 1))
+        quant("h", "ht", a, b, "qh%d" % c)
     g.vector.wait_ge(S.lw2, 16)
     quant("w2", "w2t", 0, 512, "qw2")
+
+    def issue(phase, relayed, items):
+        ph = p[phase]
+        for kind in (0, 1):
+            out = []
+            for it in items:
+                if relayed:
+                    pair, lo, w, tr = it
+                    out.append((ph["relays"][2 * pair + kind], "rin_" + phase, (ph["buf"], ph["base"] + lo), ("r" + phase, 0), w))
+                else:
+                    sem, tb, ta = target(P, phase, r, it)
+                    out.append((cores[it], sem, (ph["buf"], ph["base"] + ph["pos"][it]), (tb, ta), ph["cnt"][it]))
+            send(g, T, topo, core, kind, out, sent)
+
+    for c, calls in enumerate(p["o"]["calls"]):
+        g.wait_ge(S["qh%d" % c], 1)
+        for relayed, items in calls:
+            issue("o", relayed, items)
+
+    g.tensor.wait_ge(S.qw2, 1)
+    if own:
+        g.tensor.wait_ge(S["qh%d" % (len(hch) - 1)], 1)
+    for c, (a, b) in enumerate(gch):
+        k = arrivals(P, topo, cores, "o", r, "in%d" % c)
+        if k:
+            g.tensor.wait_ge(S["in%d" % c], k)
+        layer("w2", "h", NC - own + a, "gt", a, b, C2, "mg%d" % c, "ag%d" % c, "qg%d" % c, VEC_G)
+        quant("g", "gt", a, b, "qg%d" % c, NC + a)
+    for c, k in SENDS[r]:
+        g.wait_ge(S["qg%d" % c], 1)
+        issue("b", *p["b"]["calls"][c][k])
     g.vector.wait_ge(S.lw3, 16)
     quant("w3", "w3t", 0, 128, "qw3")
 
-    def far_send(phase):
-        sets = p["osets" if phase == "o" else "bsets"]
-        pos, cnt, base, buf = source(P, phase, r)
-        for kind in (0, 1):
-            items = []
-            for s, (a, b) in enumerate(p["owin" if phase == "o" else "bwin"]):
-                items.append((p["relays"][2 * s + kind], "rin_" + phase, (buf, base + a), ("r" + phase, 0), b - a))
-            if items:
-                send(g, T, topo, core, kind, items, sent)
-
-    def near_send(phase, chunk):
-        for call in near_calls(P, phase, r, chunk):
-            for kind in (0, 1):
-                send(g, T, topo, core, kind, [(cores[d], sem, src, (tb, ta), w) for d, (sem, tb, ta), src, w in call], sent)
-
-    g.wait_ge(S.qh0, 1)
-    far_send("o")
-    near_send("o", 0)
-    g.wait_ge(S.qh1, 1)
-    near_send("o", 1)
-
-    g.tensor.wait_ge(S.qw2, 1)
-    for c in range(2):
-        a, b = gch[c]
-        g.tensor.wait_ge(S["qh%d" % c], 1)
-        if c == 0:
-            g.tensor.wait_ge(S.qh1, 1)
-        g.tensor.wait_ge(S["in%d" % c], arrivals(P, topo, cores, "o", r, "in%d" % c))
-        products("w2", "h", NC - own + a, b - a, c, "mg")
-        drain("gt", a, b, c, C2, "mg", "ag")
-        quant("g", "gt", a, b, "qg%d" % c, NC + a)
-    if p["bsets"]:
-        g.wait_ge(S.qg1, 1)
-        far_send("b")
-        g.wait_ge(S.qg0, 1)
-        near_send("b", 0)
-        near_send("b", 1)
-    else:
-        for c in range(2):
-            g.wait_ge(S["qg%d" % c], 1)
-            near_send("b", c)
-
     g.tensor.wait_ge(S.qw3, 1)
+    if own:
+        g.tensor.wait_ge(S.qg0, 1)
     for c, (a, b) in enumerate(p["ych"]):
-        g.tensor.wait_ge(S["qg%d" % c], 1)
-        if c == 0 and len(p["ych"]) == 1:
-            g.tensor.wait_ge(S.qg1, 1)
+        take()
         g.tensor.wait_ge(S["home%d" % c], arrivals(P, topo, cores, "b", r, "home%d" % c))
         parts = [(a, b)]
         if b - a >= 256:
@@ -335,21 +328,21 @@ def rank_core(g, core, T, topo, P, r):
             mid = min(edges, key=lambda at: abs(2 * at - a - b))
             parts = [(a, mid), (mid, b)]
         for i, (lo, hi) in enumerate(parts):
-            bank = 512 * (4 * c + i)
-            k = "%d%d" % (c, i)
-            g.tensor.matmul_mx(T.ps[:, bank:bank + hi - lo], T.qw3[:], T.sw3[:], T.qg[:, own + lo:own + hi],
+            k, src = "%d%d" % (c, i), T.ps[:, bank(i):bank(i) + hi - lo]
+            g.tensor.matmul_mx(src, T.qw3[:], T.sw3[:], T.qg[:, own + lo:own + hi],
                                T.sg[:, own + lo:own + hi], True, True).then_inc(S["my" + k], 1)
             cp, st = (g.vector, g.sync) if i else (g.scalar, g.scalar)
             cp.wait_ge(S["my" + k], 1)
             if i:
-                g.vector.tensor_copy(T.yt[:, lo:hi], T.ps[:, bank:bank + hi - lo]).then_inc(S["cy" + k], 1)
+                g.vector.tensor_copy(T.yt[:, lo:hi], src).then_inc(S["cy" + k], 1)
             else:
-                g.scalar.activation(T.yt[:, lo:hi], T.ps[:, bank:bank + hi - lo], ActivationFunctionType.Copy).then_inc(S["cy" + k], 1)
+                g.scalar.activation(T.yt[:, lo:hi], src, ActivationFunctionType.Copy).then_inc(S["cy" + k], 1)
             st.wait_ge(S["cy" + k], 1)
             rs = runs(p["apos"], p, lo, hi)
             for at, o, w in rs:
                 st.dma_start(T.y[:, o:o + w], T.yt[:, at:at + w]).then_inc(S["st" + k], 16)
             g.wait_ge(S["st" + k], 16 * len(rs))
+        freed.append("cy%d0" % c)
     g.wait_ge(S.sent, sent[0])
 
 
@@ -360,5 +353,5 @@ def rank_program(g, core, T, topo):
         rank_core(g, core, T, topo, P, r)
         return
     for j in range(len(P)):
-        if core in P[j]["relays"][:4]:
+        if core in P[j]["o"]["relays"]:
             relay_core(g, core, T, topo, P, j)

from concourse.bass import DstId, RemoteDMATransfer
from concourse.mybir import dt, AluOpType, ActivationFunctionType

NC = 512
SIM_CORES = 112
C1, C2 = 0.041, 0.037

OUT = [
    [[[[5]]], [[[4]]], [[[1]]]],
    [[[[5]]], [[[3]]], [[[0]], [[4]]]],
    [[[[0]]], [[[4]]], [[[1]]]],
    [[[[2]], [[1]]], [[[5]]]],
    [[[[1]]], [[[2]]], [[[0]]]],
    [[[[2]]], [[[0, 1]]], [[[3]]]],
]
BACK = [
    [[[[4]]], [[[2]]], [[[1]], [[5]]]],
    [[[[4]]], [[[0]], [[2]]], [[[5], [3]]]],
    [[[[4]]], [[[5]], [[3]]]],
    [[], [[[5]]], [[[1]]]],
    [[[[2]]], [[[1]], [[0]]]],
    [[[[3]]], [[[1]]], [[[0]]]],
]
SENDS = [
    [(0, 0), (2, 0), (2, 1), (1, 0)],
    [(0, 0), (2, 0), (1, 1), (1, 0)],
    [(0, 0), (1, 0), (1, 1)],
    [(2, 0), (1, 0)],
    [(0, 0), (1, 1), (1, 0)],
    [(1, 0), (2, 0), (0, 0)],
]
VIA_O = [[], [], [0], [], [], []]
VIA_B = [[4], [], [], [], [], []]
FIRST_O = [0, 1, 0, 0, 1, 1]
FIRST_B = [1, 1, 0, 0, 1, 1]
VEC_H0, VEC_H, VEC_G = (1,), (1, 3), (2,)
MAXCH = 3

F8 = "float8_e4m3fn_x4"
SCRATCH = {
    "xt": ("sbuf", [128, 2048], "bfloat16"), "w1t": ("sbuf", [128, 2048], "bfloat16"),
    "w2t": ("sbuf", [128, 2048], "bfloat16"), "w3t": ("sbuf", [128, 512], "bfloat16"),
    "ht": ("sbuf", [128, 2048], "bfloat16"), "gt": ("sbuf", [128, 2048], "bfloat16"),
    "yt": ("sbuf", [128, 512], "float32"),
    "ps": ("psum", [128, 4096], "float32"),
}
for _n, _w in (("x", 512), ("w1", 512), ("w2", 512), ("w3", 128), ("h", 1024), ("g", 1024), ("ro", 512), ("rb", 512)):
    SCRATCH["q" + _n] = ("sbuf", [128, _w], F8)
    SCRATCH["s" + _n] = ("sbuf", [128, _w], "uint8")

SEMAPHORES = (["lw10", "lw11", "lw2", "lw3", "qw10", "qw11", "qw2", "qw3", "home0", "home1", "rin_o", "rin_b", "sent"]
              + ["%s%d" % (p, c) for p in ("lx", "qx", "qh", "qg", "in") for c in range(MAXCH)]
              + ["%s%d%d" % (p, c, i) for p in ("mh", "ah", "mg", "ag") for c in range(MAXCH) for i in range(4)]
              + ["%s%d%d" % (p, c, i) for p in ("my", "cy", "st") for c in range(2) for i in range(2)])


def classes(dests, cnt):
    out = {}
    for d in dests:
        out.setdefault(cnt[d], []).append(d)
    return sorted(out.values(), key=lambda ds: -cnt[ds[0]] * len(ds))


def lay_out(chunks, cnt, relayed, at, first, last):
    pos, bounds, calls, pair = {}, [], [], 0
    start = at
    at += first
    for c, chunk in enumerate(chunks):
        calls.append([])
        for call in chunk:
            for tr in call:
                for d in tr:
                    pos[d] = at
                    at += cnt[d]
            if relayed[call[0][0]]:
                w = max(sum(cnt[d] for d in tr) for tr in call)
                items = []
                for tr in call:
                    items.append((pair, min(pos[tr[0]], at - w), w, tr))
                    pair += 1
                calls[-1].append((True, items))
            else:
                calls[-1].append((False, [tr[0] for tr in call]))
        if c == len(chunks) - 1:
            at += last
        bounds.append((start, at))
        start = at
    return pos, bounds, calls


def make_plan(T, topo):
    CNT, cores = T.tables["CNT"], T.cores
    n = len(cores)
    P = []
    for r in range(n):
        far = [i != r and not topo.may_write(cores[r], cores[i]) for i in range(n)]
        oc, bc, own = CNT[r], [CNT[i][r] for i in range(n)], CNT[r][r]
        p = {"far": far, "own": own, "off": [sum(oc[:e]) for e in range(n + 1)], "o": {}, "b": {}}
        o, b = p["o"], p["b"]
        o["cnt"], o["base"], o["buf"] = oc, 0, "h"
        o["pos"], o["ch"], o["calls"] = lay_out(OUT[r], oc, [far[i] or i in VIA_O[r] for i in range(n)], 0, 0, own)
        o["pos"][r] = NC - own
        b["cnt"], b["base"], b["buf"] = bc, NC, "g"
        b["pos"], b["ch"], b["calls"] = lay_out(BACK[r], bc, [far[i] or i in VIA_B[r] for i in range(n)], 0, own, 0)
        b["pos"][r] = 0
        b["of"] = {d: c for c, chunk in enumerate(BACK[r]) for call in chunk for tr in call for d in tr}
        p["apos"], at, cut = {}, 0, 0
        for f in (True, False):
            for d in range(n):
                if oc[d] and d != r and far[d] == f:
                    p["apos"][d] = at
                    at += oc[d]
            cut = at if f else cut
        p["apos"][r] = at
        p["ych"] = [(cut, NC), (0, cut)] if cut else [(0, NC)]
        probe = [i for i in range(n) if far[i]][0]
        rel = sorted([c for c in range(SIM_CORES) if topo.chip(c) == topo.chip(cores[r])
                      and c != cores[r] and topo.may_write(c, cores[probe])],
                     key=lambda c: (topo.die(c) == topo.die(cores[r]), c))
        o["relays"] = rel[2 * FIRST_O[r]:] + rel[:2 * FIRST_O[r]]
        b["relays"] = rel[2 * FIRST_B[r]:] + rel[:2 * FIRST_B[r]]
        P.append(p)
    return P


def runs(pos, p, a, b):
    out = []
    for at, d in sorted((at, d) for d, at in pos.items() if p["o"]["cnt"][d]):
        lo, hi = max(a, at), min(b, at + p["o"]["cnt"][d])
        if lo >= hi:
            continue
        o = p["off"][d] + lo - at
        if out and out[-1][0] + out[-1][2] == lo and out[-1][1] + out[-1][2] == o:
            out[-1][2] += hi - lo
        else:
            out.append([lo, o, hi - lo])
    return out


def ones(m):
    return bin(m).count("1")


def deal(mask, k):
    bits = [b for b in range(mask.bit_length()) if mask >> b & 1]
    return [sum(1 << b for b in bits[i::k]) for i in range(k)]


def view(T, kind, name, a, b):
    if kind == 0:
        return T["q" + name][:, a:b].bitcast(dt.uint8)
    return T["s" + name][:, a:b]


def send(g, T, topo, core, kind, items, sent):
    k = len(items)
    ms = [deal(topo.mask(core, it[0]), k)[i] for i, it in enumerate(items)]
    sent[0] += sum(ones(m) for m in ms)
    if k == 1:
        dst, sem, (sb, sa), (tb, ta), w = items[0]
        rid, pid, _ = topo.addr(dst)
        g.remote_dma(view(T, kind, tb, ta, ta + w), view(T, kind, sb, sa, sa + w), T.sem[sem], T.sem.sent, pid, rid, ms[0])
        return
    tr = []
    for m, (dst, sem, (sb, sa), (tb, ta), w) in zip(ms, items):
        rid, pid, _ = topo.addr(dst)
        tr.append(RemoteDMATransfer(dst_ids=[DstId(rid=rid, pnc=pid)], dma_engine_mask=m, remote_sem=T.sem[sem],
                                    src=view(T, kind, sb, sa, sa + w), dst=view(T, kind, tb, ta, ta + w)))
    g.remote_dma_fused(tr, local_sem=T.sem.sent)


def target(P, phase, r, d):
    q = P[d]
    if phase == "o":
        return "in%d" % q["b"]["of"][r], "h", NC - q["own"] + q["b"]["pos"][r]
    return "home%d" % (1 if q["far"][r] else 0), "g", q["own"] + q["apos"][r]


def arrivals(P, topo, cores, phase, d, sem):
    tot = 0
    for r in range(len(P)):
        if r == d or not P[r][phase]["cnt"][d] or target(P, phase, r, d)[0] != sem:
            continue
        for calls in P[r][phase]["calls"]:
            for relayed, items in calls:
                if not relayed and d in items:
                    tot += 2 * (ones(topo.mask(cores[r], cores[d])) // len(items))
                for pair, lo, w, tr in items if relayed else []:
                    if d in tr:
                        cl = [c for c in classes(tr, P[r][phase]["cnt"]) if d in c][0]
                        for kind in (0, 1):
                            tot += ones(topo.mask(P[r][phase]["relays"][2 * pair + kind], cores[d])) // len(cl)
    return tot


def relay_core(g, core, T, topo, P, r):
    p, cores, sent = P[r], T.cores, [0]
    for phase in ("o", "b"):
        ph = p[phase]
        k = ph["relays"].index(core)
        for relayed, items in [c for cs in ph["calls"] for c in cs]:
            for i, (pair, lo, w, tr) in enumerate(items if relayed else []):
                if pair != k // 2:
                    continue
                g.wait_ge(T.sem["rin_" + phase], ones(deal(topo.mask(cores[r], core), len(items))[i]))
                for cl in classes(tr, ph["cnt"]):
                    out = []
                    for d in cl:
                        sem, tb, ta = target(P, phase, r, d)
                        out.append((cores[d], sem, ("r" + phase, ph["pos"][d] - lo), (tb, ta), ph["cnt"][d]))
                    send(g, T, topo, core, k % 2, out, sent)
    if sent[0]:
        g.wait_ge(T.sem.sent, sent[0])


def rank_core(g, core, T, topo, P, r):
    p, cores, sent, S = P[r], T.cores, [0], T.sem
    hch, gch, own = p["o"]["ch"], p["b"]["ch"], p["own"]
    relu = ActivationFunctionType.Relu

    nx = []
    for c in range(len(hch)):
        rs = runs(p["o"]["pos"], p, *hch[c])
        nx.append(16 * len(rs))
        for at, o, w in rs:
            g.sync.dma_start(T.xt[:, 4 * at:4 * (at + w)], T.x[:, 4 * o:4 * (o + w)]).then_inc(S["lx%d" % c], 16)
    for c in range(2):
        g.scalar.dma_start(T.w1t[:, 1024 * c:1024 * (c + 1)], T.w1[:, 1024 * c:1024 * (c + 1)]).then_inc(S["lw1%d" % c], 16)
    g.sync.dma_start(T.w2t[:], T.w2[:]).then_inc(S.lw2, 16)
    g.sync.wait_ge(S.qg0, 1)
    g.sync.dma_start(T.w3t[:], T.w3[:]).then_inc(S.lw3, 16)

    def quant(name, tile, a, b, sem, at=None):
        at = a if at is None else at
        g.vector.quantize_mx(T["q" + name][:, at:at + b - a], T["s" + name][:, at:at + b - a],
                             T[tile][:, 4 * a:4 * b]).then_inc(S[sem], 1)

    freed = []

    def bank(i):
        return 512 * (4 * (len(freed) % 2) + i)

    def take():
        if len(freed) >= 2:
            g.tensor.wait_ge(S[freed[-2]], 1)

    def layer(w, buf, at, tile, a, b, const, m, s, q, vec, gate=None, ahead=None):
        n = b - a
        take()
        for i in range(4):
            if gate and i in gate:
                g.tensor.wait_ge(S[gate[i]], 1)
            g.tensor.matmul_mx(T.ps[:, bank(i):bank(i) + n], T["q" + w][:, 128 * i:128 * i + 128], T["s" + w][:, 128 * i:128 * i + 128],
                               T["q" + buf][:, at:at + n], T["s" + buf][:, at:at + n], True, True).then_inc(S["%s%d" % (m, i)], 1)
        if ahead:
            ahead()
        for i in range(4):
            out, src = T[tile][:, 4 * a + i:4 * b:4], T.ps[:, bank(i):bank(i) + n]
            e = g.vector if i in vec else g.scalar
            e.wait_ge(S["%s%d" % (m, i)], 1)
            if i in vec:
                g.vector.tensor_scalar(out, src, 0.0, const, AluOpType.max, AluOpType.mult).then_inc(S["%s%d" % (s, i)], 1)
            else:
                g.scalar.activation(out, src, relu, scale=const).then_inc(S["%s%d" % (s, i)], 1)
        for i in range(4):
            g.vector.wait_ge(S["%s%d" % (s, i)], 1)
        freed.append(q)

    def quant_x(c):
        if c < len(hch):
            g.vector.wait_ge(S["lx%d" % c], nx[c])
            quant("x", "xt", hch[c][0], hch[c][1], "qx%d" % c)

    quant_x(0)
    for c in range(2):
        g.vector.wait_ge(S["lw1%d" % c], 16)
        quant("w1", "w1t", 256 * c, 256 * c + 256, "qw1%d" % c)
    for c, (a, b) in enumerate(hch):
        g.tensor.wait_ge(S["qx%d" % c], 1)
        layer("w1", "x", a, "ht", a, b, C1, "mh%d" % c, "ah%d" % c, "qh%d" % c, VEC_H if c else VEC_H0,
              gate={} if c else {0: "qw10", 2: "qw11"}, ahead=lambda: quant_x(c + 1))
        quant("h", "ht", a, b, "qh%d" % c)
    g.vector.wait_ge(S.lw2, 16)
    quant("w2", "w2t", 0, 512, "qw2")

    def issue(phase, relayed, items):
        ph = p[phase]
        for kind in (0, 1):
            out = []
            for it in items:
                if relayed:
                    pair, lo, w, tr = it
                    out.append((ph["relays"][2 * pair + kind], "rin_" + phase, (ph["buf"], ph["base"] + lo), ("r" + phase, 0), w))
                else:
                    sem, tb, ta = target(P, phase, r, it)
                    out.append((cores[it], sem, (ph["buf"], ph["base"] + ph["pos"][it]), (tb, ta), ph["cnt"][it]))
            send(g, T, topo, core, kind, out, sent)

    for c, calls in enumerate(p["o"]["calls"]):
        g.wait_ge(S["qh%d" % c], 1)
        for relayed, items in calls:
            issue("o", relayed, items)

    g.tensor.wait_ge(S.qw2, 1)
    if own:
        g.tensor.wait_ge(S["qh%d" % (len(hch) - 1)], 1)
    for c, (a, b) in enumerate(gch):
        k = arrivals(P, topo, cores, "o", r, "in%d" % c)
        if k:
            g.tensor.wait_ge(S["in%d" % c], k)
        layer("w2", "h", NC - own + a, "gt", a, b, C2, "mg%d" % c, "ag%d" % c, "qg%d" % c, VEC_G)
        quant("g", "gt", a, b, "qg%d" % c, NC + a)
    for c, k in SENDS[r]:
        g.wait_ge(S["qg%d" % c], 1)
        issue("b", *p["b"]["calls"][c][k])
    g.vector.wait_ge(S.lw3, 16)
    quant("w3", "w3t", 0, 128, "qw3")

    g.tensor.wait_ge(S.qw3, 1)
    if own:
        g.tensor.wait_ge(S.qg0, 1)
    for c, (a, b) in enumerate(p["ych"]):
        take()
        g.tensor.wait_ge(S["home%d" % c], arrivals(P, topo, cores, "b", r, "home%d" % c))
        parts = [(a, b)]
        if b - a >= 256:
            edges = [at for at in p["apos"].values() if a + 128 <= at <= b - 128] or [(a + b) // 2]
            mid = min(edges, key=lambda at: abs(2 * at - a - b))
            parts = [(a, mid), (mid, b)]
        for i, (lo, hi) in enumerate(parts):
            k, src = "%d%d" % (c, i), T.ps[:, bank(i):bank(i) + hi - lo]
            g.tensor.matmul_mx(src, T.qw3[:], T.sw3[:], T.qg[:, own + lo:own + hi],
                               T.sg[:, own + lo:own + hi], True, True).then_inc(S["my" + k], 1)
            cp, st = (g.vector, g.sync) if i else (g.scalar, g.scalar)
            cp.wait_ge(S["my" + k], 1)
            if i:
                g.vector.tensor_copy(T.yt[:, lo:hi], src).then_inc(S["cy" + k], 1)
            else:
                g.scalar.activation(T.yt[:, lo:hi], src, ActivationFunctionType.Copy).then_inc(S["cy" + k], 1)
            st.wait_ge(S["cy" + k], 1)
            rs = runs(p["apos"], p, lo, hi)
            for at, o, w in rs:
                st.dma_start(T.y[:, o:o + w], T.yt[:, at:at + w]).then_inc(S["st" + k], 16)
            g.wait_ge(S["st" + k], 16 * len(rs))
        freed.append("cy%d0" % c)
    g.wait_ge(S.sent, sent[0])


def rank_program(g, core, T, topo):
    P = make_plan(T, topo)
    r = T.rank_of(core)
    if r is not None:
        rank_core(g, core, T, topo, P, r)
        return
    for j in range(len(P)):
        if core in P[j]["o"]["relays"]:
            relay_core(g, core, T, topo, P, j)
